import numpy as np
import ml_dtypes


def mxq(x, axis, fmt="e4m3"):
    dtype, down = {"e4m3": (ml_dtypes.float8_e4m3fn, 7), "e5m2": (ml_dtypes.float8_e5m2, 14)}[fmt]
    v = np.moveaxis(np.asarray(x, np.float32).astype(ml_dtypes.bfloat16).astype(np.float64), axis, -1)
    blocks = v.reshape(v.shape[:-1] + (-1, 32))
    amax = np.abs(blocks).max(-1, keepdims=True)
    byte = np.maximum(np.where(amax > 0, np.frexp(amax)[1] - 1 + 127, 0) - down, 1)
    scale = np.exp2(byte - 127.0)
    codes = (blocks / scale).astype(np.float32).astype(dtype).astype(np.float64)
    return np.moveaxis((codes * scale).reshape(v.shape), -1, axis)


WIDE = False


def mx_kscale(k):
    if not WIDE:
        return np.ones(k)
    levels = np.array([30, -30])
    if k % 512:
        return np.exp2(np.random.permutation(np.resize(levels, k // 32))).repeat(32)
    a = np.empty((k // 512, 16))
    for p in range(k // 512):
        a[p, :8] = np.random.permutation(np.resize(levels, 8))
        for g in range(8):
            far = levels[np.abs(levels - a[p, g]) >= 10]
            a[p, g + 8] = far[np.random.randint(len(far))]
    return np.exp2(a.ravel()).repeat(32)


def f64(x):
    return np.asarray(x).astype(np.float64)


def striped(idx):
    return np.tile(np.asarray(idx).reshape(-1, 16).T, (8, 1)).astype(np.uint16)


def unstriped(offs):
    return offs[:16].T.reshape(-1).astype(np.int64)


E2M1 = np.array([0.0, 0.5, 1.0, 1.5, 2.0, 3.0, 4.0, 6.0, -0.0, -0.5, -1.0, -1.5, -2.0, -3.0, -4.0, -6.0])


def pack_weight(w, fmt):
    k, n = w.shape
    w = f64(np.asarray(w, np.float32).astype(ml_dtypes.bfloat16)).reshape(k // 32, 32, n)
    amax = np.abs(w).max(1)
    if fmt in ("e4m3", "e5m2"):
        byte = np.frexp(amax)[1] - 1 + 127 - (7 if fmt == "e4m3" else 14)
    else:
        mant, ex = np.frexp(amax / 6.0)
        byte = np.where(mant > 0.5, ex, ex - 1) + 127
    byte = np.clip(np.where(amax > 0, byte, 1), 1, 254)
    scaled = (w * np.exp2(127.0 - byte)[:, None, :]).reshape(k, n).astype(np.float32)
    by_word = np.ascontiguousarray(scaled.reshape(k // 512, 128, 4, n).transpose(0, 1, 3, 2))
    if fmt in ("e4m3", "e5m2"):
        words = by_word.astype(ml_dtypes.float8_e4m3fn if fmt == "e4m3" else ml_dtypes.float8_e5m2).view(np.uint8)
    else:
        c = by_word.astype(ml_dtypes.float4_e2m1fn).view(np.uint8) & 0xF
        words = (c[..., 0::2] | (c[..., 1::2] << 4)).reshape(k // 512, 128, 2 * n)
    return np.ascontiguousarray(words), np.ascontiguousarray(byte.astype(np.uint8).reshape(k // 512, 16, n))


def unpack_weight(words, scales, fmt):
    g, _, n = scales.shape
    words = np.ascontiguousarray(words).reshape(g, 128, n, -1)
    if fmt in ("e4m3", "e5m2"):
        vals = words.view(ml_dtypes.float8_e4m3fn if fmt == "e4m3" else ml_dtypes.float8_e5m2).astype(np.float64)
    else:
        nib = np.empty((g, 128, n, 4), np.uint8)
        nib[..., 0::2] = words & 0xF
        nib[..., 1::2] = words >> 4
        vals = E2M1[nib]
    vals = vals * np.repeat(np.exp2(scales.astype(np.float64) - 127.0), 8, axis=1)[..., None]
    return vals.transpose(0, 1, 3, 2).reshape(g * 512, n)


K, T, J, R, C, O, N, L, E = 512, 1024, 256, 512, 512, 256, 256, 512, 128


def setup_inputs():
    n = np.random.standard_normal
    idx = np.random.permutation(T)[:J]
    idx2 = np.random.permutation(C)[:J]
    idx3 = np.random.permutation(C)[:J]
    idx4 = np.random.permutation(C)[:O]
    idx5 = np.random.permutation(C)[:O]
    idx6 = np.random.permutation(O)[:E]
    idx7 = np.random.permutation(O)[:E]
    fk = mx_kscale(K)
    fr = mx_kscale(R)
    fl = mx_kscale(L)
    xtp = pack_weight(n((K, T)) / fk[:, None], "e2m1")
    wp = pack_weight(n((K, R)) * 1 / np.sqrt(K) * fk[:, None] * fr, "e4m3")
    w2p = pack_weight(n((K, R)) * 1 / np.sqrt(K) * fk[:, None] * fr, "e5m2")
    wbp = pack_weight(n((R, N)) * 1 / np.sqrt(R) / fr[:, None], "e2m1")
    sxp = pack_weight(n((L, O)) / fl[:, None], "e4m3")
    wsp = pack_weight(n((L, N)) * 1 / np.sqrt(L) * fl[:, None], "e4m3")
    return {
        "xt_words": xtp[0],
        "xt_scales": xtp[1],
        "w_words": wp[0],
        "w_scales": wp[1],
        "w2_words": w2p[0],
        "w2_scales": w2p[1],
        "wb_words": wbp[0],
        "wb_scales": wbp[1],
        "sx_words": sxp[0],
        "sx_scales": sxp[1],
        "ws_words": wsp[0],
        "ws_scales": wsp[1],
        "offs": striped(idx),
        "offs2": striped(idx2),
        "offs3": striped(idx3),
        "offs4": striped(idx4),
        "offs5": striped(idx5),
        "offs6": striped(idx6),
        "offs7": striped(idx7),
    }


def reference(xt_words, xt_scales, w_words, w_scales, w2_words, w2_scales, wb_words, wb_scales, sx_words, sx_scales, ws_words, ws_scales, offs, offs2, offs3, offs4, offs5, offs6, offs7):
    idx = unstriped(offs)
    idx2 = unstriped(offs2)
    idx3 = unstriped(offs3)
    idx4 = unstriped(offs4)
    idx5 = unstriped(offs5)
    idx6 = unstriped(offs6)
    idx7 = unstriped(offs7)
    xtu = unpack_weight(xt_words, xt_scales, "e2m1")
    wu = unpack_weight(w_words, w_scales, "e4m3")
    w2u = unpack_weight(w2_words, w2_scales, "e5m2")
    wbu = unpack_weight(wb_words, wb_scales, "e2m1")
    sxu = unpack_weight(sx_words, sx_scales, "e4m3")
    wsu = unpack_weight(ws_words, ws_scales, "e4m3")
    xtidxg = xtu[:, idx]
    a = wu.T @ xtidxg
    b = w2u.T @ xtidxg
    pw = np.zeros((R, C))
    pw[:, idx2] = a
    pv = np.zeros((R, C))
    pv[:, idx3] = b
    hid = np.abs(pw[:, idx4] - pv[:, idx5])
    hidq = mxq(hid, 0, "e5m2")
    p = wbu.T @ hidq + wsu.T @ sxu
    y = np.maximum(p[:, idx6], p[:, idx7])
    return y

@@ -1,0 +1,201 @@
+from contextlib import ExitStack
+
+import concourse.mybir as mybir
+
+K, T, J, R, C, O, N, L, E = 512, 1024, 256, 512, 512, 256, 256, 512, 128
+FLOPS = 2 * (2 * K * R * J + R * N * O + L * N * O)
+
+F32 = mybir.dt.float32
+BF16 = mybir.dt.bfloat16
+I32 = mybir.dt.int32
+U32 = mybir.dt.uint32
+U16 = mybir.dt.uint16
+U8 = mybir.dt.uint8
+E4M3 = mybir.dt.float8_e4m3fn_x4
+E5M2 = mybir.dt.float8_e5m2_x4
+E2M1 = mybir.dt.float4_e2m1fn_x4
+COPY = mybir.ActivationFunctionType.Copy
+ABS = mybir.ActivationFunctionType.Abs
+SUB = mybir.AluOpType.subtract
+MAX = mybir.AluOpType.max
+
+P = 128
+PACK = 4
+BANK = 512
+HALF = O // 2
+
+
+def tile_list_twow_twoboards_skip_bestoftwo_kernel(
+    tc, xt_words, xt_scales, w_words, w_scales, w2_words, w2_scales, wb_words, wb_scales,
+    sx_words, sx_scales, ws_words, ws_scales, offs, offs2, offs3, offs4, offs5, offs6, offs7, out,
+):
+    nc = tc.nc
+    with ExitStack() as ctx:
+        lists = ctx.enter_context(tc.tile_pool(name="lists", bufs=1))
+        sb = ctx.enter_context(tc.tile_pool(name="sb", bufs=1))
+        ps = ctx.enter_context(tc.psum_pool(name="ps", bufs=1))
+
+        def load_list(name, src):
+            tile = lists.tile(list(src.shape), U16, name=name)
+            nc.sync.dma_start(tile[:], src)
+            return tile
+
+        def load_words(queue, name, src, dtype, width):
+            tile = sb.tile([P, width], dtype, name=name, align_bytes=64)
+            queue.dma_start(tile[:].bitcast(I32), src.bitcast(I32))
+            return tile
+
+        def load_scales(queues, tile, col, src):
+            width = src.shape[2]
+            for q, queue in enumerate(queues):
+                queue.dma_start(
+                    tile[32 * q : 32 * q + 4, col : col + width].bitcast(I32),
+                    src[0, 4 * q : 4 * q + 4, :].bitcast(I32),
+                )
+
+        def fp8_rows(src):
+            return src[0].rearrange("p n t -> p (n t)")
+
+        x_sc = sb.tile([P, T], U8, name="x_sc", align_bytes=64)
+        w_sc = sb.tile([P, R], U8, name="w_sc", align_bytes=64)
+        w2_sc = sb.tile([P, R], U8, name="w2_sc", align_bytes=64)
+        late_sc = sb.tile([P, 3 * N], U8, name="late_sc", align_bytes=64)
+        nc.vector.memset(x_sc[:].bitcast(I32), 0)
+        nc.vector.memset(w_sc[:].bitcast(I32), 0)
+        nc.vector.memset(w2_sc[:].bitcast(I32), 0)
+        nc.vector.memset(late_sc[:].bitcast(I32), 0)
+
+        sy, sc = nc.sync, nc.scalar
+        idx = load_list("idx", offs)
+        x_w = load_words(sy, "x_w", xt_words[0], U16, T)
+        w_w = load_words(sc, "w_w", fp8_rows(w_words), U32, R)
+        load_scales((sc, sy, sc, sy), x_sc, 0, xt_scales)
+        load_scales((sc, sy, sc, sy), w_sc, 0, w_scales)
+        idx2 = load_list("idx2", offs2)
+        w2_w = load_words(sy, "w2_w", fp8_rows(w2_words), U32, R)
+        load_scales((sy, sy, sy, sy), w2_sc, 0, w2_scales)
+        idx4 = load_list("idx4", offs4)
+        idx3 = load_list("idx3", offs3)
+        idx5 = load_list("idx5", offs5)
+        ws_w = load_words(sy, "ws_w", fp8_rows(ws_words), U32, N)
+        sx_w = load_words(sy, "sx_w", fp8_rows(sx_words), U32, O)
+        load_scales((sy,) * 4, late_sc, 0, ws_scales)
+        load_scales((sy,) * 4, late_sc, N, sx_scales)
+        wb_w = load_words(sy, "wb_w", wb_words[0], U16, N)
+        load_scales((sy,) * 4, late_sc, 2 * N, wb_scales)
+        idx6 = load_list("idx6", offs6)
+        idx7 = load_list("idx7", offs7)
+
+        pw = [sb.tile([P, C], F32, name=f"pw{t}") for t in range(PACK)]
+        pv = [sb.tile([P, C], F32, name=f"pv{t}") for t in range(PACK)]
+
+        xg_w = sb.tile([P, J], U16, name="xg_w", align_bytes=64)
+        xg_sc = sb.tile([P, J], U8, name="xg_sc", align_bytes=64)
+        nc.vector.tensor_copy(xg_w[:], x_w[:].indirect(idx[:]))
+        nc.vector.tensor_copy(xg_sc[:], x_sc[:].indirect(idx[:]))
+
+        def deal(engine, order, name, words, scales):
+            dealt_w = sb.tile([P, R], U32, name=name + "_dw", align_bytes=64)
+            dealt_sc = sb.tile([P, R], U8, name=name + "_dsc", align_bytes=64)
+            engine.tensor_copy(
+                dealt_w[:].bitcast(I32).rearrange("p (t m) -> " + order, t=PACK),
+                words[:].bitcast(I32).rearrange("p (m t) -> " + order, t=PACK),
+            )
+            engine.tensor_copy(
+                dealt_sc[:].rearrange("p (t m) -> " + order, t=PACK),
+                scales[:].rearrange("p (m t) -> " + order, t=PACK),
+            )
+            return dealt_w, dealt_sc
+
+        def first_stage(bank, col, dealt, fmt, t):
+            nc.tensor.matmul_mx(
+                bank[:, col : col + J],
+                lhsT=dealt[0][:, P * t : P * (t + 1)].bitcast(fmt), lhsT_scale=dealt[1][:, P * t : P * (t + 1)],
+                rhs=xg_w[:].bitcast(E2M1), rhs_scale=xg_sc[:], start=True, stop=True,
+            )
+
+        for board in pw:
+            nc.vector.memset(board[:], 0.0)
+        for board in pv:
+            nc.gpsimd.memset(board[:], 0.0)
+
+        banks = [ps.tile([P, BANK], F32, name=f"bank{i}") for i in range(6)]
+        p_bank = [ps.tile([P, BANK], F32, name=f"p_bank{i}") for i in range(2)]
+        w_dealt = deal(nc.vector, "p m t", "w", w_w, w_sc)
+        for t in range(PACK):
+            first_stage(banks[t], 0, w_dealt, E4M3, t)
+        w2_dealt = deal(nc.gpsimd, "p t m", "w2", w2_w, w2_sc)
+        for t in range(PACK):
+            first_stage(banks[4 + t % 2], J * (t // 2), w2_dealt, E5M2, t)
+        for i in range(2):
+            nc.tensor.matmul_mx(
+                p_bank[i][:, 0:O],
+                lhsT=ws_w[:, P * i : P * (i + 1)].bitcast(E4M3), lhsT_scale=late_sc[:, P * i : P * (i + 1)],
+                rhs=sx_w[:].bitcast(E4M3), rhs_scale=late_sc[:, N : N + O], start=True, stop=False,
+            )
+
+        a = [sb.tile([P, J], F32, name=f"a{t}") for t in range(PACK)]
+        b02 = sb.tile([P, 2 * J], F32, name="b02")
+        b13 = sb.tile([P, 2 * J], F32, name="b13")
+        got = [sb.tile([P, O], F32, name=f"got{t}") for t in range(PACK)]
+        diff = sb.tile([P, PACK, O], F32, name="diff")
+
+        def v_put(board, where, src):
+            nc.vector.tensor_copy(board[:].indirect(where[:]), src)
+
+        def s_put(board, where, src):
+            nc.scalar.activation(board[:].indirect(where[:]), src, COPY)
+
+        def s_get(t):
+            nc.scalar.activation(got[t][:], pw[t][:].indirect(idx4[:]), COPY)
+
+        def v_diff(t, lo, hi):
+            nc.vector.tensor_tensor(diff[:, t, lo:hi], pv[t][:].indirect(idx5[:, lo // 16 : hi // 16]), got[t][:, lo:hi], SUB)
+
+        for t in (0, 2):
+            nc.vector.tensor_copy(a[t][:], banks[t][:, 0:J])
+            nc.scalar.activation(a[t + 1][:], banks[t + 1][:, 0:J], COPY)
+            v_put(pw[t], idx2, a[t][:])
+            s_put(pw[t + 1], idx2, a[t + 1][:])
+        nc.vector.tensor_copy(b02[:], banks[4][:])
+        for t in (0, 2, 1, 3):
+            s_get(t)
+        nc.scalar.activation(b13[:], banks[5][:], COPY)
+        v_put(pv[0], idx3, b02[:, 0:J])
+        s_put(pv[1], idx3, b13[:, 0:J])
+        v_put(pv[2], idx3, b02[:, J : 2 * J])
+        s_put(pv[3], idx3, b13[:, J : 2 * J])
+        for t in (0, 2, 1):
+            v_diff(t, 0, O)
+
+        hid = sb.tile([P, O, PACK], BF16, name="hid", align_bytes=64)
+        hid_w = sb.tile([P, O], U32, name="hid_w", align_bytes=64)
+        hid_sc = sb.tile([P, O], U8, name="hid_sc", align_bytes=64)
+        for h in range(2):
+            v_diff(3, HALF * h, HALF * (h + 1))
+        for h in range(2):
+            cols = slice(HALF * h, HALF * (h + 1))
+            nc.scalar.activation(hid[:, cols, :], diff[:, :, cols].rearrange("p t o -> p o t"), ABS)
+        for h in range(2):
+            cols = slice(HALF * h, HALF * (h + 1))
+            nc.vector.quantize_mx(hid_w[:, cols].bitcast(E5M2), hid_sc[:, cols], hid[:, cols, :].rearrange("p o t -> p (o t)"))
+            for i in range(2):
+                nc.tensor.matmul_mx(
+                    p_bank[i][:, cols],
+                    lhsT=wb_w[:, P * i : P * (i + 1)].bitcast(E2M1), lhsT_scale=late_sc[:, 2 * N + P * i : 2 * N + P * (i + 1)],
+                    rhs=hid_w[:, cols].bitcast(E5M2), rhs_scale=hid_sc[:, cols], start=False, stop=(h == 1),
+                )
+
+        p_sb = [sb.tile([P, O], F32, name=f"p_sb{i}") for i in range(2)]
+        first = [sb.tile([P, E], F32, name=f"first{i}") for i in range(2)]
+        second = [sb.tile([P, E], F32, name=f"second{i}") for i in range(2)]
+        best = [sb.tile([P, E], F32, name=f"best{i}") for i in range(2)]
+        nc.vector.tensor_copy(p_sb[0][:], p_bank[0][:, 0:O])
+        nc.scalar.activation(p_sb[1][:], p_bank[1][:, 0:O], COPY)
+        nc.vector.tensor_copy(first[0][:], p_sb[0][:].indirect(idx6[:]))
+        nc.vector.tensor_copy(second[0][:], p_sb[0][:].indirect(idx7[:]))
+        nc.scalar.activation(first[1][:], p_sb[1][:].indirect(idx6[:]), COPY)
+        nc.scalar.activation(second[1][:], p_sb[1][:].indirect(idx7[:]), COPY)
+        for i, queue in enumerate((nc.sync, nc.scalar)):
+            nc.vector.tensor_tensor(best[i][:], first[i][:], second[i][:], MAX)
+            queue.dma_start(out[P * i : P * (i + 1), :], best[i][:])

@@ -114,10 +114,8 @@ def tile_list_twow_twoboards_skip_bestoftwo_kernel(
                 rhs=xg_w[:].bitcast(E2M1), rhs_scale=xg_sc[:], start=True, stop=True,
             )
 
-        for board in pw:
+        for board in pw + pv:
             nc.vector.memset(board[:], 0.0)
-        for board in pv:
-            nc.gpsimd.memset(board[:], 0.0)
 
         banks = [ps.tile([P, BANK], F32, name=f"bank{i}") for i in range(6)]
         p_bank = [ps.tile([P, BANK], F32, name=f"p_bank{i}") for i in range(2)]
@@ -158,14 +156,14 @@ def tile_list_twow_twoboards_skip_bestoftwo_kernel(
             v_put(pw[t], idx2, a[t][:])
             s_put(pw[t + 1], idx2, a[t + 1][:])
         nc.vector.tensor_copy(b02[:], banks[4][:])
-        for t in (0, 2, 1, 3):
+        for t in range(PACK):
             s_get(t)
         nc.scalar.activation(b13[:], banks[5][:], COPY)
         v_put(pv[0], idx3, b02[:, 0:J])
         s_put(pv[1], idx3, b13[:, 0:J])
         v_put(pv[2], idx3, b02[:, J : 2 * J])
         s_put(pv[3], idx3, b13[:, J : 2 * J])
-        for t in (0, 2, 1):
+        for t in (0, 1, 2):
             v_diff(t, 0, O)
 
         hid = sb.tile([P, O, PACK], BF16, name="hid", align_bytes=64)
@@ -173,9 +171,10 @@ def tile_list_twow_twoboards_skip_bestoftwo_kernel(
         hid_sc = sb.tile([P, O], U8, name="hid_sc", align_bytes=64)
         for h in range(2):
             v_diff(3, HALF * h, HALF * (h + 1))
+        nc.scalar.activation(hid[:, :, 0:2], diff[:, 0:2, :].rearrange("p t o -> p o t"), ABS)
         for h in range(2):
             cols = slice(HALF * h, HALF * (h + 1))
-            nc.scalar.activation(hid[:, cols, :], diff[:, :, cols].rearrange("p t o -> p o t"), ABS)
+            nc.scalar.activation(hid[:, cols, 2:4], diff[:, 2:4, cols].rearrange("p t o -> p o t"), ABS)
         for h in range(2):
             cols = slice(HALF * h, HALF * (h + 1))
             nc.vector.quantize_mx(hid_w[:, cols].bitcast(E5M2), hid_sc[:, cols], hid[:, cols, :].rearrange("p o t -> p (o t)"))

@@ -45,44 +45,40 @@ def tile_list_twow_twoboards_skip_bestoftwo_kernel(
             queue.dma_start(tile[:].bitcast(I32), src.bitcast(I32))
             return tile
 
-        def load_scales(queues, tile, col, src):
-            width = src.shape[2]
+        def load_quadrant(queue, tile, src, q):
+            rows = src[0, 4 * q : 4 * q + 4, :].bitcast(I32)
+            queue.dma_start(tile[32 * q : 32 * (q + 1), :].bitcast(I32), rows.unsqueeze(0).to_broadcast([8, 4, src.shape[2] // 4]))
+
+        def load_scales(queues, name, src):
+            tile = sb.tile([P, src.shape[2]], U8, name=name, align_bytes=64)
             for q, queue in enumerate(queues):
-                queue.dma_start(
-                    tile[32 * q : 32 * q + 4, col : col + width].bitcast(I32),
-                    src[0, 4 * q : 4 * q + 4, :].bitcast(I32),
-                )
+                load_quadrant(queue, tile, src, q)
+            return tile
 
         def fp8_rows(src):
             return src[0].rearrange("p n t -> p (n t)")
 
-        x_sc = sb.tile([P, T], U8, name="x_sc", align_bytes=64)
-        w_sc = sb.tile([P, R], U8, name="w_sc", align_bytes=64)
-        w2_sc = sb.tile([P, R], U8, name="w2_sc", align_bytes=64)
-        late_sc = sb.tile([P, 3 * N], U8, name="late_sc", align_bytes=64)
-        nc.vector.memset(x_sc[:].bitcast(I32), 0)
-        nc.vector.memset(w_sc[:].bitcast(I32), 0)
-        nc.vector.memset(w2_sc[:].bitcast(I32), 0)
-        nc.vector.memset(late_sc[:].bitcast(I32), 0)
-
         sy, sc = nc.sync, nc.scalar
         idx = load_list("idx", offs)
+        x_sc = load_scales((sc, sy, sc, sy), "x_sc", xt_scales)
         x_w = load_words(sy, "x_w", xt_words[0], U16, T)
+        w_sc = sb.tile([P, R], U8, name="w_sc", tag="w_sc", align_bytes=64)
+        load_quadrant(sc, w_sc, w_scales, 0)
         w_w = load_words(sc, "w_w", fp8_rows(w_words), U32, R)
-        load_scales((sc, sy, sc, sy), x_sc, 0, xt_scales)
-        load_scales((sc, sy, sc, sy), w_sc, 0, w_scales)
-        idx2 = load_list("idx2", offs2)
+        for q, queue in ((1, sy), (2, sc), (3, sy)):
+            load_quadrant(queue, w_sc, w_scales, q)
         w2_w = load_words(sy, "w2_w", fp8_rows(w2_words), U32, R)
-        load_scales((sy, sy, sy, sy), w2_sc, 0, w2_scales)
+        w2_sc = load_scales((sy,) * 4, "w2_sc", w2_scales)
+        idx2 = load_list("idx2", offs2)
         idx4 = load_list("idx4", offs4)
         idx3 = load_list("idx3", offs3)
         idx5 = load_list("idx5", offs5)
         ws_w = load_words(sy, "ws_w", fp8_rows(ws_words), U32, N)
         sx_w = load_words(sy, "sx_w", fp8_rows(sx_words), U32, O)
-        load_scales((sy,) * 4, late_sc, 0, ws_scales)
-        load_scales((sy,) * 4, late_sc, N, sx_scales)
+        ws_sc = load_scales((sy,) * 4, "ws_sc", ws_scales)
+        sx_sc = load_scales((sy,) * 4, "sx_sc", sx_scales)
         wb_w = load_words(sy, "wb_w", wb_words[0], U16, N)
-        load_scales((sy,) * 4, late_sc, 2 * N, wb_scales)
+        wb_sc = load_scales((sy,) * 4, "wb_sc", wb_scales)
         idx6 = load_list("idx6", offs6)
         idx7 = load_list("idx7", offs7)
 
@@ -91,11 +87,11 @@ def tile_list_twow_twoboards_skip_bestoftwo_kernel(
 
         xg_w = sb.tile([P, J], U16, name="xg_w", align_bytes=64)
         xg_sc = sb.tile([P, J], U8, name="xg_sc", align_bytes=64)
-        nc.vector.tensor_copy(xg_w[:], x_w[:].indirect(idx[:]))
         nc.vector.tensor_copy(xg_sc[:], x_sc[:].indirect(idx[:]))
+        nc.vector.tensor_copy(xg_w[:], x_w[:].indirect(idx[:]))
 
-        def deal(engine, order, name, words, scales):
-            dealt_w = sb.tile([P, R], U32, name=name + "_dw", align_bytes=64)
+        def deal(engine, order, name, words, scales, tag):
+            dealt_w = sb.tile([P, R], U32, name=name + "_dw", tag=tag, align_bytes=64)
             dealt_sc = sb.tile([P, R], U8, name=name + "_dsc", align_bytes=64)
             engine.tensor_copy(
                 dealt_w[:].bitcast(I32).rearrange("p (t m) -> " + order, t=PACK),
@@ -114,23 +110,19 @@ def tile_list_twow_twoboards_skip_bestoftwo_kernel(
                 rhs=xg_w[:].bitcast(E2M1), rhs_scale=xg_sc[:], start=True, stop=True,
             )
 
-        for board in pw + pv:
-            nc.vector.memset(board[:], 0.0)
+        for board in pw:
+            nc.vector.memset(board[:, 0 : C // 2 + 1], 0.0)
+            nc.vector.memset(board[:, C // 2 + 1 : C], 0.0)
+        for board in pv:
+            nc.gpsimd.memset(board[:], 0.0)
 
-        banks = [ps.tile([P, BANK], F32, name=f"bank{i}") for i in range(6)]
-        p_bank = [ps.tile([P, BANK], F32, name=f"p_bank{i}") for i in range(2)]
-        w_dealt = deal(nc.vector, "p m t", "w", w_w, w_sc)
+        banks = [ps.tile([P, BANK], F32, name=f"bank{i}", tag=f"bank{i}") for i in range(6)]
+        w_dealt = deal(nc.vector, "p m t", "w", w_w, w_sc, "w_dw")
         for t in range(PACK):
             first_stage(banks[t], 0, w_dealt, E4M3, t)
-        w2_dealt = deal(nc.gpsimd, "p t m", "w2", w2_w, w2_sc)
-        for t in range(PACK):
+        w2_dealt = deal(nc.vector, "p m t", "w2", w2_w, w2_sc, "w2_dw")
+        for t in (0, 2, 1, 3):
             first_stage(banks[4 + t % 2], J * (t // 2), w2_dealt, E5M2, t)
-        for i in range(2):
-            nc.tensor.matmul_mx(
-                p_bank[i][:, 0:O],
-                lhsT=ws_w[:, P * i : P * (i + 1)].bitcast(E4M3), lhsT_scale=late_sc[:, P * i : P * (i + 1)],
-                rhs=sx_w[:].bitcast(E4M3), rhs_scale=late_sc[:, N : N + O], start=True, stop=False,
-            )
 
         a = [sb.tile([P, J], F32, name=f"a{t}") for t in range(PACK)]
         b02 = sb.tile([P, 2 * J], F32, name="b02")
@@ -150,15 +142,15 @@ def tile_list_twow_twoboards_skip_bestoftwo_kernel(
         def v_diff(t, lo, hi):
             nc.vector.tensor_tensor(diff[:, t, lo:hi], pv[t][:].indirect(idx5[:, lo // 16 : hi // 16]), got[t][:, lo:hi], SUB)
 
+        for t in range(PACK):
+            nc.scalar.activation(a[t][:], banks[t][:, 0:J], COPY)
         for t in (0, 2):
-            nc.vector.tensor_copy(a[t][:], banks[t][:, 0:J])
-            nc.scalar.activation(a[t + 1][:], banks[t + 1][:, 0:J], COPY)
             v_put(pw[t], idx2, a[t][:])
             s_put(pw[t + 1], idx2, a[t + 1][:])
         nc.vector.tensor_copy(b02[:], banks[4][:])
+        nc.vector.tensor_copy(b13[:], banks[5][:])
         for t in range(PACK):
             s_get(t)
-        nc.scalar.activation(b13[:], banks[5][:], COPY)
         v_put(pv[0], idx3, b02[:, 0:J])
         s_put(pv[1], idx3, b13[:, 0:J])
         v_put(pv[2], idx3, b02[:, J : 2 * J])
@@ -166,31 +158,46 @@ def tile_list_twow_twoboards_skip_bestoftwo_kernel(
         for t in (0, 1, 2):
             v_diff(t, 0, O)
 
-        hid = sb.tile([P, O, PACK], BF16, name="hid", align_bytes=64)
-        hid_w = sb.tile([P, O], U32, name="hid_w", align_bytes=64)
-        hid_sc = sb.tile([P, O], U8, name="hid_sc", align_bytes=64)
-        for h in range(2):
-            v_diff(3, HALF * h, HALF * (h + 1))
-        nc.scalar.activation(hid[:, :, 0:2], diff[:, 0:2, :].rearrange("p t o -> p o t"), ABS)
-        for h in range(2):
-            cols = slice(HALF * h, HALF * (h + 1))
-            nc.scalar.activation(hid[:, cols, 2:4], diff[:, 2:4, cols].rearrange("p t o -> p o t"), ABS)
-        for h in range(2):
-            cols = slice(HALF * h, HALF * (h + 1))
-            nc.vector.quantize_mx(hid_w[:, cols].bitcast(E5M2), hid_sc[:, cols], hid[:, cols, :].rearrange("p o t -> p (o t)"))
+        halves = [slice(HALF * h, HALF * (h + 1)) for h in range(2)]
+        p_bank = [[ps.tile([P, BANK], F32, name=f"p_bank{h}{i}", tag=f"bank{2 * h + i}") for i in range(2)] for h in range(2)]
+        for h, cols in enumerate(halves):
             for i in range(2):
                 nc.tensor.matmul_mx(
-                    p_bank[i][:, cols],
-                    lhsT=wb_w[:, P * i : P * (i + 1)].bitcast(E2M1), lhsT_scale=late_sc[:, 2 * N + P * i : 2 * N + P * (i + 1)],
-                    rhs=hid_w[:, cols].bitcast(E5M2), rhs_scale=hid_sc[:, cols], start=False, stop=(h == 1),
+                    p_bank[h][i][:, 0:HALF],
+                    lhsT=ws_w[:, P * i : P * (i + 1)].bitcast(E4M3), lhsT_scale=ws_sc[:, P * i : P * (i + 1)],
+                    rhs=sx_w[:, cols].bitcast(E4M3), rhs_scale=sx_sc[:, cols], start=True, stop=False,
                 )
-
+        pairs = [sb.tile([P, 2, HALF, 2], BF16, name=f"pairs{h}") for h in range(2)]
+        hid = [sb.tile([P, HALF * PACK], BF16, name=f"hid{h}", align_bytes=64) for h in range(2)]
+        hid_w = sb.tile([P, O], U32, name="hid_w", align_bytes=64)
+        hid_sc = sb.tile([P, O], U8, name="hid_sc", align_bytes=64)
         p_sb = [sb.tile([P, O], F32, name=f"p_sb{i}") for i in range(2)]
+        for cols in halves:
+            v_diff(3, cols.start, cols.stop)
+        for u in range(2):
+            for h, cols in enumerate(halves):
+                nc.scalar.activation(pairs[h][:, u, :, :], diff[:, 2 * u : 2 * u + 2, cols].rearrange("p t o -> p o t"), ABS)
+        for h in range(2):
+            nc.vector.tensor_copy(
+                hid[h][:].bitcast(I32).rearrange("p (o u) -> p o u", u=2),
+                pairs[h][:].rearrange("p u o e -> p u (o e)").bitcast(I32).rearrange("p u o -> p o u"),
+            )
+        for h, cols in enumerate(halves):
+            nc.vector.quantize_mx(hid_w[:, cols].bitcast(E5M2), hid_sc[:, cols], hid[h][:])
+            for i in range(2):
+                nc.tensor.matmul_mx(
+                    p_bank[h][i][:, 0:HALF],
+                    lhsT=wb_w[:, P * i : P * (i + 1)].bitcast(E2M1), lhsT_scale=wb_sc[:, P * i : P * (i + 1)],
+                    rhs=hid_w[:, cols].bitcast(E5M2), rhs_scale=hid_sc[:, cols], start=False, stop=True,
+                )
+        for i in range(2):
+            nc.scalar.activation(p_sb[i][:, halves[0]], p_bank[0][i][:, 0:HALF], COPY)
+        nc.vector.tensor_copy(p_sb[0][:, halves[1]], p_bank[1][0][:, 0:HALF])
+        nc.scalar.activation(p_sb[1][:, halves[1]], p_bank[1][1][:, 0:HALF], COPY)
+
         first = [sb.tile([P, E], F32, name=f"first{i}") for i in range(2)]
         second = [sb.tile([P, E], F32, name=f"second{i}") for i in range(2)]
         best = [sb.tile([P, E], F32, name=f"best{i}") for i in range(2)]
-        nc.vector.tensor_copy(p_sb[0][:], p_bank[0][:, 0:O])
-        nc.scalar.activation(p_sb[1][:], p_bank[1][:, 0:O], COPY)
         nc.vector.tensor_copy(first[0][:], p_sb[0][:].indirect(idx6[:]))
         nc.vector.tensor_copy(second[0][:], p_sb[0][:].indirect(idx7[:]))
         nc.scalar.activation(first[1][:], p_sb[1][:].indirect(idx6[:]), COPY)

from contextlib import ExitStack

import concourse.mybir as mybir

K, T, J, R, C, O, N, L, E = 512, 1024, 256, 512, 512, 256, 256, 512, 128
FLOPS = 2 * (2 * K * R * J + R * N * O + L * N * O)

F32 = mybir.dt.float32
BF16 = mybir.dt.bfloat16
I32 = mybir.dt.int32
U32 = mybir.dt.uint32
U16 = mybir.dt.uint16
U8 = mybir.dt.uint8
E4M3 = mybir.dt.float8_e4m3fn_x4
E5M2 = mybir.dt.float8_e5m2_x4
E2M1 = mybir.dt.float4_e2m1fn_x4
COPY = mybir.ActivationFunctionType.Copy
ABS = mybir.ActivationFunctionType.Abs
SUB = mybir.AluOpType.subtract
MAX = mybir.AluOpType.max

P = 128
PACK = 4
BANK = 512
HALF = O // 2


def tile_list_twow_twoboards_skip_bestoftwo_kernel(
    tc, xt_words, xt_scales, w_words, w_scales, w2_words, w2_scales, wb_words, wb_scales,
    sx_words, sx_scales, ws_words, ws_scales, offs, offs2, offs3, offs4, offs5, offs6, offs7, out,
):
    nc = tc.nc
    with ExitStack() as ctx:
        lists = ctx.enter_context(tc.tile_pool(name="lists", bufs=1))
        sb = ctx.enter_context(tc.tile_pool(name="sb", bufs=1))
        ps = ctx.enter_context(tc.psum_pool(name="ps", bufs=1))

        def load_list(name, src):
            tile = lists.tile(list(src.shape), U16, name=name)
            nc.sync.dma_start(tile[:], src)
            return tile

        def load_words(queue, name, src, dtype, width):
            tile = sb.tile([P, width], dtype, name=name, align_bytes=64)
            queue.dma_start(tile[:].bitcast(I32), src.bitcast(I32))
            return tile

        def load_quadrant(queue, tile, src, q):
            rows = src[0, 4 * q : 4 * q + 4, :].bitcast(I32)
            queue.dma_start(tile[32 * q : 32 * (q + 1), :].bitcast(I32), rows.unsqueeze(0).to_broadcast([8, 4, src.shape[2] // 4]))

        def load_scales(queues, name, src):
            tile = sb.tile([P, src.shape[2]], U8, name=name, align_bytes=64)
            for q, queue in enumerate(queues):
                load_quadrant(queue, tile, src, q)
            return tile

        def fp8_rows(src):
            return src[0].rearrange("p n t -> p (n t)")

        sy, sc = nc.sync, nc.scalar
        idx = load_list("idx", offs)
        x_sc = load_scales((sc, sy, sc, sy), "x_sc", xt_scales)
        x_w = load_words(sy, "x_w", xt_words[0], U16, T)
        w_sc = sb.tile([P, R], U8, name="w_sc", tag="w_sc", align_bytes=64)
        load_quadrant(sc, w_sc, w_scales, 0)
        w_w = load_words(sc, "w_w", fp8_rows(w_words), U32, R)
        for q, queue in ((1, sy), (2, sc), (3, sy)):
            load_quadrant(queue, w_sc, w_scales, q)
        w2_w = load_words(sy, "w2_w", fp8_rows(w2_words), U32, R)
        w2_sc = load_scales((sy,) * 4, "w2_sc", w2_scales)
        idx2 = load_list("idx2", offs2)
        idx4 = load_list("idx4", offs4)
        idx3 = load_list("idx3", offs3)
        idx5 = load_list("idx5", offs5)
        ws_w = load_words(sy, "ws_w", fp8_rows(ws_words), U32, N)
        sx_w = load_words(sy, "sx_w", fp8_rows(sx_words), U32, O)
        ws_sc = load_scales((sy,) * 4, "ws_sc", ws_scales)
        sx_sc = load_scales((sy,) * 4, "sx_sc", sx_scales)
        wb_w = load_words(sy, "wb_w", wb_words[0], U16, N)
        wb_sc = load_scales((sy,) * 4, "wb_sc", wb_scales)
        idx6 = load_list("idx6", offs6)
        idx7 = load_list("idx7", offs7)

        pw = [sb.tile([P, C], F32, name=f"pw{t}") for t in range(PACK)]
        pv = [sb.tile([P, C], F32, name=f"pv{t}") for t in range(PACK)]

        xg_w = sb.tile([P, J], U16, name="xg_w", align_bytes=64)
        xg_sc = sb.tile([P, J], U8, name="xg_sc", align_bytes=64)
        nc.vector.tensor_copy(xg_sc[:], x_sc[:].indirect(idx[:]))
        nc.vector.tensor_copy(xg_w[:], x_w[:].indirect(idx[:]))

        def deal(engine, order, name, words, scales, tag):
            dealt_w = sb.tile([P, R], U32, name=name + "_dw", tag=tag, align_bytes=64)
            dealt_sc = sb.tile([P, R], U8, name=name + "_dsc", align_bytes=64)
            engine.tensor_copy(
                dealt_w[:].bitcast(I32).rearrange("p (t m) -> " + order, t=PACK),
                words[:].bitcast(I32).rearrange("p (m t) -> " + order, t=PACK),
            )
            engine.tensor_copy(
                dealt_sc[:].rearrange("p (t m) -> " + order, t=PACK),
                scales[:].rearrange("p (m t) -> " + order, t=PACK),
            )
            return dealt_w, dealt_sc

        def first_stage(bank, col, dealt, fmt, t):
            nc.tensor.matmul_mx(
                bank[:, col : col + J],
                lhsT=dealt[0][:, P * t : P * (t + 1)].bitcast(fmt), lhsT_scale=dealt[1][:, P * t : P * (t + 1)],
                rhs=xg_w[:].bitcast(E2M1), rhs_scale=xg_sc[:], start=True, stop=True,
            )

        for board in pw:
            nc.vector.memset(board[:, 0 : C // 2 + 1], 0.0)
            nc.vector.memset(board[:, C // 2 + 1 : C], 0.0)
        for board in pv:
            nc.gpsimd.memset(board[:], 0.0)

        banks = [ps.tile([P, BANK], F32, name=f"bank{i}", tag=f"bank{i}") for i in range(6)]
        w_dealt = deal(nc.vector, "p m t", "w", w_w, w_sc, "w_dw")
        for t in range(PACK):
            first_stage(banks[t], 0, w_dealt, E4M3, t)
        w2_dealt = deal(nc.vector, "p m t", "w2", w2_w, w2_sc, "w2_dw")
        for t in (0, 2, 1, 3):
            first_stage(banks[4 + t % 2], J * (t // 2), w2_dealt, E5M2, t)

        a = [sb.tile([P, J], F32, name=f"a{t}") for t in range(PACK)]
        b02 = sb.tile([P, 2 * J], F32, name="b02")
        b13 = sb.tile([P, 2 * J], F32, name="b13")
        got = [sb.tile([P, O], F32, name=f"got{t}") for t in range(PACK)]
        diff = sb.tile([P, PACK, O], F32, name="diff")

        def v_put(board, where, src):
            nc.vector.tensor_copy(board[:].indirect(where[:]), src)

        def s_put(board, where, src):
            nc.scalar.activation(board[:].indirect(where[:]), src, COPY)

        def s_get(t):
            nc.scalar.activation(got[t][:], pw[t][:].indirect(idx4[:]), COPY)

        def v_diff(t, lo, hi):
            nc.vector.tensor_tensor(diff[:, t, lo:hi], pv[t][:].indirect(idx5[:, lo // 16 : hi // 16]), got[t][:, lo:hi], SUB)

        for t in range(PACK):
            nc.scalar.activation(a[t][:], banks[t][:, 0:J], COPY)
        for t in (0, 2):
            v_put(pw[t], idx2, a[t][:])
            s_put(pw[t + 1], idx2, a[t + 1][:])
        nc.vector.tensor_copy(b02[:], banks[4][:])
        nc.vector.tensor_copy(b13[:], banks[5][:])
        for t in range(PACK):
            s_get(t)
        v_put(pv[0], idx3, b02[:, 0:J])
        s_put(pv[1], idx3, b13[:, 0:J])
        v_put(pv[2], idx3, b02[:, J : 2 * J])
        s_put(pv[3], idx3, b13[:, J : 2 * J])
        for t in (0, 1, 2):
            v_diff(t, 0, O)

        halves = [slice(HALF * h, HALF * (h + 1)) for h in range(2)]
        p_bank = [[ps.tile([P, BANK], F32, name=f"p_bank{h}{i}", tag=f"bank{2 * h + i}") for i in range(2)] for h in range(2)]
        for h, cols in enumerate(halves):
            for i in range(2):
                nc.tensor.matmul_mx(
                    p_bank[h][i][:, 0:HALF],
                    lhsT=ws_w[:, P * i : P * (i + 1)].bitcast(E4M3), lhsT_scale=ws_sc[:, P * i : P * (i + 1)],
                    rhs=sx_w[:, cols].bitcast(E4M3), rhs_scale=sx_sc[:, cols], start=True, stop=False,
                )
        pairs = [sb.tile([P, 2, HALF, 2], BF16, name=f"pairs{h}") for h in range(2)]
        hid = [sb.tile([P, HALF * PACK], BF16, name=f"hid{h}", align_bytes=64) for h in range(2)]
        hid_w = sb.tile([P, O], U32, name="hid_w", align_bytes=64)
        hid_sc = sb.tile([P, O], U8, name="hid_sc", align_bytes=64)
        p_sb = [sb.tile([P, O], F32, name=f"p_sb{i}") for i in range(2)]
        for cols in halves:
            v_diff(3, cols.start, cols.stop)
        for u in range(2):
            for h, cols in enumerate(halves):
                nc.scalar.activation(pairs[h][:, u, :, :], diff[:, 2 * u : 2 * u + 2, cols].rearrange("p t o -> p o t"), ABS)
        for h in range(2):
            nc.vector.tensor_copy(
                hid[h][:].bitcast(I32).rearrange("p (o u) -> p o u", u=2),
                pairs[h][:].rearrange("p u o e -> p u (o e)").bitcast(I32).rearrange("p u o -> p o u"),
            )
        for h, cols in enumerate(halves):
            nc.vector.quantize_mx(hid_w[:, cols].bitcast(E5M2), hid_sc[:, cols], hid[h][:])
            for i in range(2):
                nc.tensor.matmul_mx(
                    p_bank[h][i][:, 0:HALF],
                    lhsT=wb_w[:, P * i : P * (i + 1)].bitcast(E2M1), lhsT_scale=wb_sc[:, P * i : P * (i + 1)],
                    rhs=hid_w[:, cols].bitcast(E5M2), rhs_scale=hid_sc[:, cols], start=False, stop=True,
                )
        for i in range(2):
            nc.scalar.activation(p_sb[i][:, halves[0]], p_bank[0][i][:, 0:HALF], COPY)
        nc.vector.tensor_copy(p_sb[0][:, halves[1]], p_bank[1][0][:, 0:HALF])
        nc.scalar.activation(p_sb[1][:, halves[1]], p_bank[1][1][:, 0:HALF], COPY)

        first = [sb.tile([P, E], F32, name=f"first{i}") for i in range(2)]
        second = [sb.tile([P, E], F32, name=f"second{i}") for i in range(2)]
        best = [sb.tile([P, E], F32, name=f"best{i}") for i in range(2)]
        nc.vector.tensor_copy(first[0][:], p_sb[0][:].indirect(idx6[:]))
        nc.vector.tensor_copy(second[0][:], p_sb[0][:].indirect(idx7[:]))
        nc.scalar.activation(first[1][:], p_sb[1][:].indirect(idx6[:]), COPY)
        nc.scalar.activation(second[1][:], p_sb[1][:].indirect(idx7[:]), COPY)
        for i, queue in enumerate((nc.sync, nc.scalar)):
            nc.vector.tensor_tensor(best[i][:], first[i][:], second[i][:], MAX)
            queue.dma_start(out[P * i : P * (i + 1), :], best[i][:])
